import numpy as np
import ml_dtypes


def mxq(x, axis, fmt="e4m3"):
    dtype, down = {"e4m3": (ml_dtypes.float8_e4m3fn, 7), "e5m2": (ml_dtypes.float8_e5m2, 14)}[fmt]
    v = np.moveaxis(np.asarray(x, np.float32).astype(ml_dtypes.bfloat16).astype(np.float64), axis, -1)
    blocks = v.reshape(v.shape[:-1] + (-1, 32))
    amax = np.abs(blocks).max(-1, keepdims=True)
    byte = np.maximum(np.where(amax > 0, np.frexp(amax)[1] - 1 + 127, 0) - down, 1)
    scale = np.exp2(byte - 127.0)
    codes = (blocks / scale).astype(np.float32).astype(dtype).astype(np.float64)
    return np.moveaxis((codes * scale).reshape(v.shape), -1, axis)


WIDE = False


def mx_kscale(k):
    if not WIDE:
        return np.ones(k)
    levels = np.array([10, -10, 5, -5, 0])
    if k % 512:
        return np.exp2(np.random.permutation(np.resize(levels, k // 32))).repeat(32)
    a = np.empty((k // 512, 16))
    for p in range(k // 512):
        a[p, :8] = np.random.permutation(np.resize(levels, 8))
        for g in range(8):
            far = levels[np.abs(levels - a[p, g]) >= 10]
            a[p, g + 8] = far[np.random.randint(len(far))]
    return np.exp2(a.ravel()).repeat(32)


def f64(x):
    return np.asarray(x).astype(np.float64)


def striped(idx):
    return np.tile(idx.reshape(-1, 16).T, (8, 1)).astype(np.uint16)


def unstriped(offs):
    return offs[:16].T.reshape(-1).astype(np.int64)


def striped8(idx):
    return np.concatenate([x.reshape(-1, 16).T for x in idx]).astype(np.uint16)


def runs(offs, k):
    lists = np.stack([offs[16 * r : 16 * r + 16].T.reshape(-1) for r in range(8)]).astype(np.int64)
    return lists[np.arange(k) % 512 // 64]


def pack_weight(w):
    k, n = w.shape
    w = f64(np.asarray(w, np.float32).astype(ml_dtypes.bfloat16)).reshape(k // 32, 32, n)
    amax = np.abs(w).max(1)
    byte = np.clip(np.where(amax > 0, np.frexp(amax)[1] - 1 + 127 - 7, 1), 1, 254)
    scaled = (w * np.exp2(127.0 - byte)[:, None, :]).reshape(k, n).astype(np.float32)
    words = np.ascontiguousarray(scaled.reshape(k // 512, 128, 4, n).transpose(0, 1, 3, 2)).astype(ml_dtypes.float8_e4m3fn).view(np.uint8)
    return words, np.ascontiguousarray(byte.astype(np.uint8).reshape(k // 512, 16, n))


def unpack_weight(words, scales):
    g, p, n, _ = words.shape
    vals = np.ascontiguousarray(words).view(ml_dtypes.float8_e4m3fn).astype(np.float64) * np.repeat(np.exp2(scales.astype(np.float64) - 127.0), 8, axis=1)[..., None]
    return vals.transpose(0, 1, 3, 2).reshape(g * 512, n)

def planes(y):
    n, m = y.shape
    v = y.astype(np.float32).astype(ml_dtypes.bfloat16).astype(np.float64).reshape(n // 32, 32, m)
    top = np.abs(v).max(1)
    byte = np.clip(np.where(top > 0, np.frexp(top)[1] - 1 + 127 - 7, 1), 1, 254)
    codes = (v * np.exp2(127.0 - byte)[:, None, :]).reshape(n, m).astype(np.float32).astype(ml_dtypes.float8_e4m3fn).view(np.uint8)
    words = codes.reshape(n // 512, 128, 4, m).transpose(0, 1, 3, 2)
    return np.ascontiguousarray(words), np.ascontiguousarray(byte.astype(np.uint8).reshape(n // 512, 16, m))


K, T, S, V, H, W = 512, 2048, 512, 512, 512, 256


def setup_inputs():
    n = np.random.standard_normal
    s = mx_kscale(K)[:, None]
    u = mx_kscale(S)
    packed_xT = pack_weight(n((K, T)) * s)
    packed_w1 = pack_weight(n((K, H)) / np.sqrt(K) / s)
    packed_w2 = pack_weight(n((K, H)) / np.sqrt(K) / s)
    perm = np.stack([np.random.permutation(V) for _ in range(8)])
    return {
        "x_words": packed_xT[0],
        "x_scales": packed_xT[1],
        "w1_words": packed_w1[0],
        "w1_scales": packed_w1[1],
        "w2_words": packed_w2[0],
        "w2_scales": packed_w2[1],
        "ga": (np.random.uniform(0.5, 1.5, (H, 1)) * u[:, None]).astype(np.float32),
        "gb": (np.random.uniform(0.5, 1.5, (H, 1)) / u[:, None]).astype(np.float32),
        "offs": striped(np.random.permutation(T)[:S]),
        "two": striped(np.random.permutation(T)[:V]),
        "n1": striped8(np.stack([np.random.permutation(S) for _ in range(8)])),
        "la": striped8(perm[:, :W]),
        "lb": striped8(perm[:, W:]),
    }


def reference(x_words, x_scales, w1_words, w1_scales, w2_words, w2_scales, ga, gb, offs, two, n1, la, lb):
    xq = unpack_weight(x_words, x_scales)[:, unstriped(offs)]
    a = unpack_weight(w1_words, w1_scales).T @ xq
    z = f64(ga) * (np.maximum(a, a[np.arange(H)[:, None], runs(n1, H)]))
    x_two = unpack_weight(x_words, x_scales)[:, unstriped(two)]
    b = unpack_weight(w2_words, w2_scales).T @ x_two
    z2 = f64(gb) * b
    s = 0.0625 * ((mxq(z, 0, "e4m3").T @ mxq(z2, 0, "e4m3")))
    p = s[np.arange(S)[:, None], runs(la, S)]
    qv = s[np.arange(S)[:, None], runs(lb, S)]
    hb = np.maximum(p, qv)
    ha = p - (0.5 * qv)
    d1 = np.zeros((S, V))
    d1[np.arange(S)[:, None], runs(la, S)] = ha
    out = d1.copy()
    out[np.arange(S)[:, None], runs(lb, S)] = hb
    return (out,) + planes(out)

@@ -1,0 +1,195 @@
+from contextlib import ExitStack
+
+import concourse.mybir as mybir
+
+F32 = mybir.dt.float32
+BF16 = mybir.dt.bfloat16
+I32 = mybir.dt.int32
+U32 = mybir.dt.uint32
+U16 = mybir.dt.uint16
+U8 = mybir.dt.uint8
+FP8X4 = mybir.dt.float8_e4m3fn_x4
+ALU = mybir.AluOpType
+ACT = mybir.ActivationFunctionType
+
+P = 128
+PACK = 4
+T = 2048
+S = 512
+V = 512
+H = 512
+W = 256
+HALF = 256
+FLOPS = 3 * 2 * 512 * 512 * 512
+
+
+def tile_picked_keyduel_none_po_kernel(
+    tc, x_words, x_scales, w1_words, w1_scales, w2_words, w2_scales, ga, gb, offs, two, n1, la, lb, out_0, out_1, out_2
+):
+    nc = tc.nc
+
+    def words_of(dram):
+        return dram[0].rearrange("p n t -> p (n t)").bitcast(I32)
+
+    def load_scale_rows(plane, dram, quadrants):
+        for q in quadrants:
+            rows = dram[0, 4 * q : 4 * q + 4, :].bitcast(I32)
+            nc.sync.dma_start(out=plane[32 * q : 32 * q + 32, :].bitcast(I32), in_=rows.unsqueeze(0).to_broadcast([8] + list(rows.shape)))
+
+    with ExitStack() as ctx:
+        lists = ctx.enter_context(tc.tile_pool(name="lists", bufs=1))
+        sb = ctx.enter_context(tc.tile_pool(name="sb", bufs=1))
+        ps = ctx.enter_context(tc.psum_pool(name="ps", bufs=1))
+
+        offs_t = lists.tile([P, S // 16], U16, name="offs_t")
+        two_t = lists.tile([P, V // 16], U16, name="two_t")
+        n1_t = lists.tile([P, S // 16], U16, name="n1_t")
+        la_t = lists.tile([P, W // 16], U16, name="la_t")
+        lb_t = lists.tile([P, W // 16], U16, name="lb_t")
+
+        x_w = sb.tile([P, T], U32, name="x_w", align_bytes=64)
+        x_s = sb.tile([P, T], U8, name="x_s", align_bytes=64)
+        w_raw = [sb.tile([P, H], U32, name=f"w_raw{i}", align_bytes=64) for i in range(2)]
+        ws_raw = [sb.tile([P, H], U8, name=f"ws_raw{i}", align_bytes=64) for i in range(2)]
+        w_w = [sb.tile([P, H], U32, name=f"w_w{i}", align_bytes=64) for i in range(2)]
+        w_s = [sb.tile([P, H], U8, name=f"w_s{i}", align_bytes=64) for i in range(2)]
+        ga_t = sb.tile([P, PACK], F32, name="ga_t")
+        gb_t = sb.tile([P, PACK], F32, name="gb_t")
+
+        nc.gpsimd.dma_start(out=ga_t[:], in_=ga.rearrange("(p t) o -> p (t o)", t=PACK))
+        nc.gpsimd.dma_start(out=gb_t[:], in_=gb.rearrange("(p t) o -> p (t o)", t=PACK))
+        nc.sync.dma_start(offs_t[:], offs)
+        nc.sync.dma_start(two_t[:], two)
+        load_scale_rows(x_s, x_scales, (0, 1))
+        nc.sync.dma_start(out=x_w[:].bitcast(I32), in_=words_of(x_words))
+        load_scale_rows(x_s, x_scales, (2, 3))
+        nc.sync.dma_start(out=w_raw[0][:].bitcast(I32), in_=words_of(w1_words))
+        load_scale_rows(ws_raw[0], w1_scales, range(4))
+        nc.sync.dma_start(out=w_raw[1][:].bitcast(I32), in_=words_of(w2_words))
+        load_scale_rows(ws_raw[1], w2_scales, range(4))
+        nc.sync.dma_start(n1_t[:], n1)
+        nc.sync.dma_start(la_t[:], la)
+        nc.sync.dma_start(lb_t[:], lb)
+
+        ga_abs = sb.tile([P, PACK], F32, name="ga_abs")
+        nc.scalar.activation(out=ga_abs[:], in_=ga_t[:], func=ACT.Abs)
+        twice_step = sb.tile([P, PACK], F32, name="twice_step")
+        ga_sign = sb.tile([P, PACK], F32, name="ga_sign")
+        gb_signed = sb.tile([P, PACK], F32, name="gb_signed")
+        nc.gpsimd.tensor_scalar(out=twice_step[:], in0=ga_t[:], scalar1=0.0, scalar2=2.0, op0=ALU.is_ge, op1=ALU.mult)
+        nc.gpsimd.tensor_scalar(out=ga_sign[:], in0=twice_step[:], scalar1=-1.0, scalar2=None, op0=ALU.add)
+        nc.gpsimd.tensor_tensor(out=gb_signed[:], in0=gb_t[:], in1=ga_sign[:], op=ALU.mult)
+
+        xa_w = sb.tile([P, S], U32, name="xa_w", align_bytes=64)
+        xa_s = sb.tile([P, S], U8, name="xa_s", align_bytes=64)
+        xb_w = sb.tile([P, V], U32, name="xb_w", align_bytes=64)
+        xb_s = sb.tile([P, V], U8, name="xb_s", align_bytes=64)
+
+        def deal_weights(i):
+            nc.scalar.copy(out=w_w[i][:].rearrange("p (t m) -> p m t", t=PACK), in_=w_raw[i][:].rearrange("p (m t) -> p m t", t=PACK))
+            nc.vector.tensor_copy(out=w_s[i][:].rearrange("p (t m) -> p m t", t=PACK), in_=ws_raw[i][:].rearrange("p (m t) -> p m t", t=PACK))
+
+        nc.vector.tensor_copy(xa_s[:], x_s[:].indirect(offs_t[:]))
+        nc.vector.tensor_copy(xb_s[:], x_s[:].indirect(two_t[:]))
+        deal_weights(0)
+        nc.vector.tensor_copy(xa_w[:], x_w[:].indirect(offs_t[:]))
+        nc.vector.tensor_copy(xb_w[:], x_w[:].indirect(two_t[:]))
+        deal_weights(1)
+
+        a_ps = []
+        for t in range(PACK):
+            bank = ps.tile([P, S], F32, name=f"a_ps{t}", tag=f"bank{t}")
+            cols = slice(P * t, P * (t + 1))
+            nc.tensor.matmul_mx(out=bank[:], lhsT=w_w[0][:, cols].bitcast(FP8X4), lhsT_scale=w_s[0][:, cols],
+                                rhs=xa_w[:].bitcast(FP8X4), rhs_scale=xa_s[:], start=True, stop=True)
+            a_ps.append(bank)
+        b_ps = []
+        for c in range(V // P):
+            bank = ps.tile([P, PACK, P], F32, name=f"b_ps{c}", tag=f"bank{PACK + c}")
+            keys = slice(P * c, P * (c + 1))
+            for t in range(PACK):
+                cols = slice(P * t, P * (t + 1))
+                nc.tensor.matmul_mx(out=bank[:, t, :], lhsT=w_w[1][:, cols].bitcast(FP8X4), lhsT_scale=w_s[1][:, cols],
+                                    rhs=xb_w[:, keys].bitcast(FP8X4), rhs_scale=xb_s[:, keys], start=True, stop=True)
+            b_ps.append(bank)
+
+        a_sb = [sb.tile([P, S], F32, name=f"a_sb{t}") for t in range(PACK)]
+        rival = [[sb.tile([P, HALF], F32, name=f"rival{t}_{h}") for h in range(2)] for t in range(PACK)]
+        z_planes = [sb.tile([P, PACK, HALF], BF16, name=f"z_planes{h}") for h in range(2)]
+        z_bf = sb.tile([P, PACK, P, PACK], BF16, name="z_bf", align_bytes=64)
+        z2_bf = sb.tile([P, V, PACK], BF16, name="z2_bf", align_bytes=64)
+
+        def fetch_rival(t, h):
+            window = a_sb[t][:].indirect(n1_t[:, 16 * h : 16 * (h + 1)])
+            nc.scalar.activation(out=rival[t][h][:], in_=window, func=ACT.Copy)
+
+        def larger(t, h):
+            nc.vector.tensor_tensor(out=z_planes[h][:, t, :], in0=a_sb[t][:, HALF * h : HALF * (h + 1)], in1=rival[t][h][:], op=ALU.max)
+
+        def weave(h):
+            nc.vector.tensor_copy(out=z_bf[:, :, 64 * h : 64 * (h + 1), :].rearrange("p r m t -> p m t r"),
+                                  in_=z_planes[h][:].rearrange("p t (m r) -> p m t r", r=PACK))
+
+        def weigh_b(c):
+            nc.vector.tensor_tensor(out=z2_bf[:, P * c : P * (c + 1), :], in0=b_ps[c][:].rearrange("p t n -> p n t"),
+                                    in1=gb_signed[:].unsqueeze(1).to_broadcast([P, P, PACK]), op=ALU.mult)
+
+        z_w = sb.tile([P, S], U32, name="z_w", align_bytes=64)
+        z_s = sb.tile([P, S], U8, name="z_s", align_bytes=64)
+        z2_w = sb.tile([P, V], U32, name="z2_w", align_bytes=64)
+        z2_s = sb.tile([P, V], U8, name="z2_s", align_bytes=64)
+
+        for t in range(PACK):
+            nc.scalar.activation(out=a_sb[t][:], in_=a_ps[t][:], func=ACT.Copy, scale=ga_abs[:, t : t + 1])
+            fetch_rival(t, 0)
+            larger(t, 0)
+            weigh_b(t)
+        nc.vector.quantize_mx(out=z2_w[:].bitcast(FP8X4), scales=z2_s[:], in_=z2_bf[:].rearrange("p n t -> p (n t)"))
+        weave(0)
+        for t in range(PACK):
+            fetch_rival(t, 1)
+            larger(t, 1)
+        weave(1)
+
+        scores = [sb.tile([P, V], F32, name=f"scores{r}") for r in range(PACK)]
+        first = [sb.tile([P, W], F32, name=f"first{r}") for r in range(PACK)]
+        less_half = [sb.tile([P, W], F32, name=f"less_half{r}") for r in range(PACK)]
+        winner = [sb.tile([P, W], F32, name=f"winner{r}") for r in range(PACK)]
+        result = [sb.tile([P, V], F32, name=f"result{r}") for r in range(PACK)]
+        y_bf = sb.tile([P, V, PACK], BF16, name="y_bf", align_bytes=64)
+        out_rows = out_0.rearrange("(p r) v -> r p v", r=PACK)
+
+        for r in range(PACK):
+            cols = slice(P * r, P * (r + 1))
+            nc.vector.quantize_mx(out=z_w[:, cols].bitcast(FP8X4), scales=z_s[:, cols], in_=z_bf[:, r].rearrange("p m t -> p (m t)"))
+        for r in range(PACK):
+            cols = slice(P * r, P * (r + 1))
+            bank = ps.tile([P, V], F32, name=f"s_ps{r}", tag=f"bank{PACK + r}")
+            nc.tensor.matmul_mx(out=bank[:], lhsT=z_w[:, cols].bitcast(FP8X4), lhsT_scale=z_s[:, cols],
+                                rhs=z2_w[:].bitcast(FP8X4), rhs_scale=z2_s[:], start=True, stop=True)
+            nc.scalar.activation(out=scores[r][:], in_=bank[:], func=ACT.Copy, scale=0.0625)
+            nc.scalar.activation(out=first[r][:], in_=scores[r][:].indirect(la_t[:]), func=ACT.Copy)
+            nc.scalar.activation(out=less_half[r][:], in_=scores[r][:].indirect(lb_t[:]), func=ACT.Copy, scale=-0.5)
+
+        def put_first(r):
+            nc.vector.scalar_tensor_tensor(out=winner[r][:], in0=less_half[r][:], scalar=-2.0, in1=first[r][:], op0=ALU.mult, op1=ALU.max)
+            nc.vector.tensor_tensor(out=result[r][:].indirect(la_t[:]), in0=first[r][:], in1=less_half[r][:], op=ALU.add)
+
+        def put_second(r):
+            nc.vector.tensor_copy(out=result[r][:].indirect(lb_t[:]), in_=winner[r][:])
+            nc.sync.dma_start(out=out_rows[r], in_=result[r][:])
+            nc.scalar.copy(out=y_bf[:, :, r], in_=result[r][:])
+
+        put_first(0)
+        for r in range(1, PACK):
+            put_first(r)
+            put_second(r - 1)
+        put_second(PACK - 1)
+
+        y_w = sb.tile([P, V], U32, name="y_w", align_bytes=64)
+        y_s = sb.tile([P, V], U8, name="y_s", align_bytes=64)
+        nc.vector.quantize_mx(out=y_w[:].bitcast(FP8X4), scales=y_s[:], in_=y_bf[:].rearrange("p n t -> p (n t)"))
+        nc.sync.dma_start(out=words_of(out_1), in_=y_w[:].bitcast(I32))
+        for q in range(4):
+            engine = nc.scalar if q % 2 else nc.sync
+            engine.dma_start(out=out_2[0, 4 * q : 4 * q + 4, :].bitcast(I32), in_=y_s[32 * q : 32 * q + 4, :].bitcast(I32))

@@ -31,10 +31,10 @@ def tile_picked_keyduel_none_po_kernel(
     def words_of(dram):
         return dram[0].rearrange("p n t -> p (n t)").bitcast(I32)
 
-    def load_scale_rows(plane, dram, quadrants):
-        for q in quadrants:
+    def load_scale_rows(engine, plane, dram):
+        for q in range(4):
             rows = dram[0, 4 * q : 4 * q + 4, :].bitcast(I32)
-            nc.sync.dma_start(out=plane[32 * q : 32 * q + 32, :].bitcast(I32), in_=rows.unsqueeze(0).to_broadcast([8] + list(rows.shape)))
+            engine.dma_start(out=plane[32 * q : 32 * q + 32, :].bitcast(I32), in_=rows.unsqueeze(0).to_broadcast([8] + list(rows.shape)))
 
     with ExitStack() as ctx:
         lists = ctx.enter_context(tc.tile_pool(name="lists", bufs=1))
@@ -50,7 +50,7 @@ def tile_picked_keyduel_none_po_kernel(
         x_w = sb.tile([P, T], U32, name="x_w", align_bytes=64)
         x_s = sb.tile([P, T], U8, name="x_s", align_bytes=64)
         w_raw = [sb.tile([P, H], U32, name=f"w_raw{i}", align_bytes=64) for i in range(2)]
-        ws_raw = [sb.tile([P, H], U8, name=f"ws_raw{i}", align_bytes=64) for i in range(2)]
+        ws_raw = [sb.tile([P, H], U8, name=f"ws_raw{i}", tag=f"ws_raw{i}", align_bytes=64) for i in range(2)]
         w_w = [sb.tile([P, H], U32, name=f"w_w{i}", align_bytes=64) for i in range(2)]
         w_s = [sb.tile([P, H], U8, name=f"w_s{i}", align_bytes=64) for i in range(2)]
         ga_t = sb.tile([P, PACK], F32, name="ga_t")
@@ -59,14 +59,13 @@ def tile_picked_keyduel_none_po_kernel(
         nc.gpsimd.dma_start(out=ga_t[:], in_=ga.rearrange("(p t) o -> p (t o)", t=PACK))
         nc.gpsimd.dma_start(out=gb_t[:], in_=gb.rearrange("(p t) o -> p (t o)", t=PACK))
         nc.sync.dma_start(offs_t[:], offs)
+        load_scale_rows(nc.sync, x_s, x_scales)
         nc.sync.dma_start(two_t[:], two)
-        load_scale_rows(x_s, x_scales, (0, 1))
         nc.sync.dma_start(out=x_w[:].bitcast(I32), in_=words_of(x_words))
-        load_scale_rows(x_s, x_scales, (2, 3))
         nc.sync.dma_start(out=w_raw[0][:].bitcast(I32), in_=words_of(w1_words))
-        load_scale_rows(ws_raw[0], w1_scales, range(4))
+        load_scale_rows(nc.sync, ws_raw[0], w1_scales)
         nc.sync.dma_start(out=w_raw[1][:].bitcast(I32), in_=words_of(w2_words))
-        load_scale_rows(ws_raw[1], w2_scales, range(4))
+        load_scale_rows(nc.sync, ws_raw[1], w2_scales)
         nc.sync.dma_start(n1_t[:], n1)
         nc.sync.dma_start(la_t[:], la)
         nc.sync.dma_start(lb_t[:], lb)
@@ -82,7 +81,6 @@ def tile_picked_keyduel_none_po_kernel(
 
         xa_w = sb.tile([P, S], U32, name="xa_w", align_bytes=64)
         xa_s = sb.tile([P, S], U8, name="xa_s", align_bytes=64)
-        xb_w = sb.tile([P, V], U32, name="xb_w", align_bytes=64)
         xb_s = sb.tile([P, V], U8, name="xb_s", align_bytes=64)
 
         def deal_weights(i):
@@ -91,8 +89,9 @@ def tile_picked_keyduel_none_po_kernel(
 
         nc.vector.tensor_copy(xa_s[:], x_s[:].indirect(offs_t[:]))
         nc.vector.tensor_copy(xb_s[:], x_s[:].indirect(two_t[:]))
-        deal_weights(0)
         nc.vector.tensor_copy(xa_w[:], x_w[:].indirect(offs_t[:]))
+        deal_weights(0)
+        xb_w = sb.tile([P, V], U32, name="xb_w", tag="ws_raw0", align_bytes=64)
         nc.vector.tensor_copy(xb_w[:], x_w[:].indirect(two_t[:]))
         deal_weights(1)
 
@@ -114,21 +113,25 @@ def tile_picked_keyduel_none_po_kernel(
             b_ps.append(bank)
 
         a_sb = [sb.tile([P, S], F32, name=f"a_sb{t}") for t in range(PACK)]
-        rival = [[sb.tile([P, HALF], F32, name=f"rival{t}_{h}") for h in range(2)] for t in range(PACK)]
-        z_planes = [sb.tile([P, PACK, HALF], BF16, name=f"z_planes{h}") for h in range(2)]
+        a_rows = sb.tile([P, PACK, S], F32, name="a_rows")
+        pieces = [(0, 256), (256, 384), (384, 512)]
+        rival = [sb.tile([P, PACK, hi - lo], F32, name=f"rival{lo}") for lo, hi in pieces]
         z_bf = sb.tile([P, PACK, P, PACK], BF16, name="z_bf", align_bytes=64)
         z2_bf = sb.tile([P, V, PACK], BF16, name="z2_bf", align_bytes=64)
 
         def fetch_rival(t, h):
-            window = a_sb[t][:].indirect(n1_t[:, 16 * h : 16 * (h + 1)])
-            nc.scalar.activation(out=rival[t][h][:], in_=window, func=ACT.Copy)
+            lo, hi = pieces[h]
+            window = a_sb[t][:].indirect(n1_t[:, lo // 16 : hi // 16])
+            if (t, h) == (0, 0):
+                nc.vector.tensor_copy(out=rival[h][:, t, :], in_=window)
+            else:
+                nc.scalar.activation(out=rival[h][:, t, :], in_=window, func=ACT.Copy)
 
-        def larger(t, h):
-            nc.vector.tensor_tensor(out=z_planes[h][:, t, :], in0=a_sb[t][:, HALF * h : HALF * (h + 1)], in1=rival[t][h][:], op=ALU.max)
-
-        def weave(h):
-            nc.vector.tensor_copy(out=z_bf[:, :, 64 * h : 64 * (h + 1), :].rearrange("p r m t -> p m t r"),
-                                  in_=z_planes[h][:].rearrange("p t (m r) -> p m t r", r=PACK))
+        def larger(h):
+            lo, hi = pieces[h]
+            nc.vector.tensor_tensor(out=z_bf[:, :, lo // PACK : hi // PACK, :].rearrange("p r m t -> p m t r"),
+                                    in0=a_rows[:, :, lo:hi].rearrange("p t (m r) -> p m t r", r=PACK),
+                                    in1=rival[h][:].rearrange("p t (m r) -> p m t r", r=PACK), op=ALU.max)
 
         def weigh_b(c):
             nc.vector.tensor_tensor(out=z2_bf[:, P * c : P * (c + 1), :], in0=b_ps[c][:].rearrange("p t n -> p n t"),
@@ -141,20 +144,20 @@ def tile_picked_keyduel_none_po_kernel(
 
         for t in range(PACK):
             nc.scalar.activation(out=a_sb[t][:], in_=a_ps[t][:], func=ACT.Copy, scale=ga_abs[:, t : t + 1])
-            fetch_rival(t, 0)
-            larger(t, 0)
-            weigh_b(t)
+            nc.sync.dma_start(out=a_rows[:, t, :], in_=a_sb[t][:])
+        for h in range(len(pieces)):
+            for t in range(PACK):
+                fetch_rival(t, h)
+        for c in range(V // P):
+            weigh_b(c)
         nc.vector.quantize_mx(out=z2_w[:].bitcast(FP8X4), scales=z2_s[:], in_=z2_bf[:].rearrange("p n t -> p (n t)"))
-        weave(0)
-        for t in range(PACK):
-            fetch_rival(t, 1)
-            larger(t, 1)
-        weave(1)
+        for h in range(len(pieces)):
+            larger(h)
 
         scores = [sb.tile([P, V], F32, name=f"scores{r}") for r in range(PACK)]
-        first = [sb.tile([P, W], F32, name=f"first{r}") for r in range(PACK)]
-        less_half = [sb.tile([P, W], F32, name=f"less_half{r}") for r in range(PACK)]
-        winner = [sb.tile([P, W], F32, name=f"winner{r}") for r in range(PACK)]
+        first = [sb.tile([P, 2, W], F32, name=f"first{g}") for g in range(2)]
+        less_half = [sb.tile([P, 2, W], F32, name=f"less_half{g}") for g in range(2)]
+        winner = [sb.tile([P, 2, W], F32, name=f"winner{g}") for g in range(2)]
         result = [sb.tile([P, V], F32, name=f"result{r}") for r in range(PACK)]
         y_bf = sb.tile([P, V, PACK], BF16, name="y_bf", align_bytes=64)
         out_rows = out_0.rearrange("(p r) v -> r p v", r=PACK)
@@ -168,28 +171,36 @@ def tile_picked_keyduel_none_po_kernel(
             nc.tensor.matmul_mx(out=bank[:], lhsT=z_w[:, cols].bitcast(FP8X4), lhsT_scale=z_s[:, cols],
                                 rhs=z2_w[:].bitcast(FP8X4), rhs_scale=z2_s[:], start=True, stop=True)
             nc.scalar.activation(out=scores[r][:], in_=bank[:], func=ACT.Copy, scale=0.0625)
-            nc.scalar.activation(out=first[r][:], in_=scores[r][:].indirect(la_t[:]), func=ACT.Copy)
-            nc.scalar.activation(out=less_half[r][:], in_=scores[r][:].indirect(lb_t[:]), func=ACT.Copy, scale=-0.5)
+            nc.scalar.activation(out=first[r // 2][:, r % 2, :], in_=scores[r][:].indirect(la_t[:]), func=ACT.Copy)
+            if r == 0:
+                nc.vector.tensor_scalar(out=less_half[r // 2][:, r % 2, :], in0=scores[r][:].indirect(lb_t[:]), scalar1=-0.5, scalar2=0.0, op0=ALU.mult, op1=ALU.add)
+            else:
+                nc.scalar.activation(out=less_half[r // 2][:, r % 2, :], in_=scores[r][:].indirect(lb_t[:]), func=ACT.Copy, scale=-0.5)
 
         def put_first(r):
-            nc.vector.scalar_tensor_tensor(out=winner[r][:], in0=less_half[r][:], scalar=-2.0, in1=first[r][:], op0=ALU.mult, op1=ALU.max)
-            nc.vector.tensor_tensor(out=result[r][:].indirect(la_t[:]), in0=first[r][:], in1=less_half[r][:], op=ALU.add)
+            nc.vector.tensor_tensor(out=result[r][:].indirect(la_t[:]), in0=first[r // 2][:, r % 2, :], in1=less_half[r // 2][:, r % 2, :], op=ALU.add)
 
         def put_second(r):
-            nc.vector.tensor_copy(out=result[r][:].indirect(lb_t[:]), in_=winner[r][:])
+            nc.vector.tensor_copy(out=result[r][:].indirect(lb_t[:]), in_=winner[r // 2][:, r % 2, :])
             nc.sync.dma_start(out=out_rows[r], in_=result[r][:])
-            nc.scalar.copy(out=y_bf[:, :, r], in_=result[r][:])
+            cols = slice(0, V) if r < 2 else slice(HALF, V)
+            nc.scalar.copy(out=y_bf[:, cols, r], in_=result[r][:, cols])
 
-        put_first(0)
-        for r in range(1, PACK):
-            put_first(r)
-            put_second(r - 1)
-        put_second(PACK - 1)
+        for g in range(2):
+            put_first(2 * g)
+            nc.vector.scalar_tensor_tensor(out=winner[g][:], in0=less_half[g][:], scalar=-2.0, in1=first[g][:], op0=ALU.mult, op1=ALU.max)
+            put_first(2 * g + 1)
+            put_second(2 * g)
+            put_second(2 * g + 1)
 
         y_w = sb.tile([P, V], U32, name="y_w", align_bytes=64)
         y_s = sb.tile([P, V], U8, name="y_s", align_bytes=64)
-        nc.vector.quantize_mx(out=y_w[:].bitcast(FP8X4), scales=y_s[:], in_=y_bf[:].rearrange("p n t -> p (n t)"))
-        nc.sync.dma_start(out=words_of(out_1), in_=y_w[:].bitcast(I32))
+        halves = [slice(HALF * h, HALF * (h + 1)) for h in range(2)]
+        for r in (2, 3):
+            nc.vector.tensor_copy(out=y_bf[:, :HALF, r], in_=result[r][:, :HALF])
+        for cols in halves:
+            nc.vector.quantize_mx(out=y_w[:, cols].bitcast(FP8X4), scales=y_s[:, cols], in_=y_bf[:, cols, :].rearrange("p n t -> p (n t)"))
+            nc.sync.dma_start(out=words_of(out_1)[:, cols], in_=y_w[:, cols].bitcast(I32))
         for q in range(4):
             engine = nc.scalar if q % 2 else nc.sync
             engine.dma_start(out=out_2[0, 4 * q : 4 * q + 4, :].bitcast(I32), in_=y_s[32 * q : 32 * q + 4, :].bitcast(I32))

from contextlib import ExitStack

import concourse.mybir as mybir

F32 = mybir.dt.float32
BF16 = mybir.dt.bfloat16
I32 = mybir.dt.int32
U32 = mybir.dt.uint32
U16 = mybir.dt.uint16
U8 = mybir.dt.uint8
FP8X4 = mybir.dt.float8_e4m3fn_x4
ALU = mybir.AluOpType
ACT = mybir.ActivationFunctionType

P = 128
PACK = 4
T = 2048
S = 512
V = 512
H = 512
W = 256
HALF = 256
FLOPS = 3 * 2 * 512 * 512 * 512


def tile_picked_keyduel_none_po_kernel(
    tc, x_words, x_scales, w1_words, w1_scales, w2_words, w2_scales, ga, gb, offs, two, n1, la, lb, out_0, out_1, out_2
):
    nc = tc.nc

    def words_of(dram):
        return dram[0].rearrange("p n t -> p (n t)").bitcast(I32)

    def load_scale_rows(engine, plane, dram):
        for q in range(4):
            rows = dram[0, 4 * q : 4 * q + 4, :].bitcast(I32)
            engine.dma_start(out=plane[32 * q : 32 * q + 32, :].bitcast(I32), in_=rows.unsqueeze(0).to_broadcast([8] + list(rows.shape)))

    with ExitStack() as ctx:
        lists = ctx.enter_context(tc.tile_pool(name="lists", bufs=1))
        sb = ctx.enter_context(tc.tile_pool(name="sb", bufs=1))
        ps = ctx.enter_context(tc.psum_pool(name="ps", bufs=1))

        offs_t = lists.tile([P, S // 16], U16, name="offs_t")
        two_t = lists.tile([P, V // 16], U16, name="two_t")
        n1_t = lists.tile([P, S // 16], U16, name="n1_t")
        la_t = lists.tile([P, W // 16], U16, name="la_t")
        lb_t = lists.tile([P, W // 16], U16, name="lb_t")

        x_w = sb.tile([P, T], U32, name="x_w", align_bytes=64)
        x_s = sb.tile([P, T], U8, name="x_s", align_bytes=64)
        w_raw = [sb.tile([P, H], U32, name=f"w_raw{i}", align_bytes=64) for i in range(2)]
        ws_raw = [sb.tile([P, H], U8, name=f"ws_raw{i}", tag=f"ws_raw{i}", align_bytes=64) for i in range(2)]
        w_w = [sb.tile([P, H], U32, name=f"w_w{i}", align_bytes=64) for i in range(2)]
        w_s = [sb.tile([P, H], U8, name=f"w_s{i}", align_bytes=64) for i in range(2)]
        ga_t = sb.tile([P, PACK], F32, name="ga_t")
        gb_t = sb.tile([P, PACK], F32, name="gb_t")

        nc.gpsimd.dma_start(out=ga_t[:], in_=ga.rearrange("(p t) o -> p (t o)", t=PACK))
        nc.gpsimd.dma_start(out=gb_t[:], in_=gb.rearrange("(p t) o -> p (t o)", t=PACK))
        nc.sync.dma_start(offs_t[:], offs)
        load_scale_rows(nc.sync, x_s, x_scales)
        nc.sync.dma_start(two_t[:], two)
        nc.sync.dma_start(out=x_w[:].bitcast(I32), in_=words_of(x_words))
        nc.sync.dma_start(out=w_raw[0][:].bitcast(I32), in_=words_of(w1_words))
        load_scale_rows(nc.sync, ws_raw[0], w1_scales)
        nc.sync.dma_start(out=w_raw[1][:].bitcast(I32), in_=words_of(w2_words))
        load_scale_rows(nc.sync, ws_raw[1], w2_scales)
        nc.sync.dma_start(n1_t[:], n1)
        nc.sync.dma_start(la_t[:], la)
        nc.sync.dma_start(lb_t[:], lb)

        ga_abs = sb.tile([P, PACK], F32, name="ga_abs")
        nc.scalar.activation(out=ga_abs[:], in_=ga_t[:], func=ACT.Abs)
        twice_step = sb.tile([P, PACK], F32, name="twice_step")
        ga_sign = sb.tile([P, PACK], F32, name="ga_sign")
        gb_signed = sb.tile([P, PACK], F32, name="gb_signed")
        nc.gpsimd.tensor_scalar(out=twice_step[:], in0=ga_t[:], scalar1=0.0, scalar2=2.0, op0=ALU.is_ge, op1=ALU.mult)
        nc.gpsimd.tensor_scalar(out=ga_sign[:], in0=twice_step[:], scalar1=-1.0, scalar2=None, op0=ALU.add)
        nc.gpsimd.tensor_tensor(out=gb_signed[:], in0=gb_t[:], in1=ga_sign[:], op=ALU.mult)

        xa_w = sb.tile([P, S], U32, name="xa_w", align_bytes=64)
        xa_s = sb.tile([P, S], U8, name="xa_s", align_bytes=64)
        xb_s = sb.tile([P, V], U8, name="xb_s", align_bytes=64)

        def deal_weights(i):
            nc.scalar.copy(out=w_w[i][:].rearrange("p (t m) -> p m t", t=PACK), in_=w_raw[i][:].rearrange("p (m t) -> p m t", t=PACK))
            nc.vector.tensor_copy(out=w_s[i][:].rearrange("p (t m) -> p m t", t=PACK), in_=ws_raw[i][:].rearrange("p (m t) -> p m t", t=PACK))

        nc.vector.tensor_copy(xa_s[:], x_s[:].indirect(offs_t[:]))
        nc.vector.tensor_copy(xb_s[:], x_s[:].indirect(two_t[:]))
        nc.vector.tensor_copy(xa_w[:], x_w[:].indirect(offs_t[:]))
        deal_weights(0)
        xb_w = sb.tile([P, V], U32, name="xb_w", tag="ws_raw0", align_bytes=64)
        nc.vector.tensor_copy(xb_w[:], x_w[:].indirect(two_t[:]))
        deal_weights(1)

        a_ps = []
        for t in range(PACK):
            bank = ps.tile([P, S], F32, name=f"a_ps{t}", tag=f"bank{t}")
            cols = slice(P * t, P * (t + 1))
            nc.tensor.matmul_mx(out=bank[:], lhsT=w_w[0][:, cols].bitcast(FP8X4), lhsT_scale=w_s[0][:, cols],
                                rhs=xa_w[:].bitcast(FP8X4), rhs_scale=xa_s[:], start=True, stop=True)
            a_ps.append(bank)
        b_ps = []
        for c in range(V // P):
            bank = ps.tile([P, PACK, P], F32, name=f"b_ps{c}", tag=f"bank{PACK + c}")
            keys = slice(P * c, P * (c + 1))
            for t in range(PACK):
                cols = slice(P * t, P * (t + 1))
                nc.tensor.matmul_mx(out=bank[:, t, :], lhsT=w_w[1][:, cols].bitcast(FP8X4), lhsT_scale=w_s[1][:, cols],
                                    rhs=xb_w[:, keys].bitcast(FP8X4), rhs_scale=xb_s[:, keys], start=True, stop=True)
            b_ps.append(bank)

        a_sb = [sb.tile([P, S], F32, name=f"a_sb{t}") for t in range(PACK)]
        a_rows = sb.tile([P, PACK, S], F32, name="a_rows")
        pieces = [(0, 256), (256, 384), (384, 512)]
        rival = [sb.tile([P, PACK, hi - lo], F32, name=f"rival{lo}") for lo, hi in pieces]
        z_bf = sb.tile([P, PACK, P, PACK], BF16, name="z_bf", align_bytes=64)
        z2_bf = sb.tile([P, V, PACK], BF16, name="z2_bf", align_bytes=64)

        def fetch_rival(t, h):
            lo, hi = pieces[h]
            window = a_sb[t][:].indirect(n1_t[:, lo // 16 : hi // 16])
            if (t, h) == (0, 0):
                nc.vector.tensor_copy(out=rival[h][:, t, :], in_=window)
            else:
                nc.scalar.activation(out=rival[h][:, t, :], in_=window, func=ACT.Copy)

        def larger(h):
            lo, hi = pieces[h]
            nc.vector.tensor_tensor(out=z_bf[:, :, lo // PACK : hi // PACK, :].rearrange("p r m t -> p m t r"),
                                    in0=a_rows[:, :, lo:hi].rearrange("p t (m r) -> p m t r", r=PACK),
                                    in1=rival[h][:].rearrange("p t (m r) -> p m t r", r=PACK), op=ALU.max)

        def weigh_b(c):
            nc.vector.tensor_tensor(out=z2_bf[:, P * c : P * (c + 1), :], in0=b_ps[c][:].rearrange("p t n -> p n t"),
                                    in1=gb_signed[:].unsqueeze(1).to_broadcast([P, P, PACK]), op=ALU.mult)

        z_w = sb.tile([P, S], U32, name="z_w", align_bytes=64)
        z_s = sb.tile([P, S], U8, name="z_s", align_bytes=64)
        z2_w = sb.tile([P, V], U32, name="z2_w", align_bytes=64)
        z2_s = sb.tile([P, V], U8, name="z2_s", align_bytes=64)

        for t in range(PACK):
            nc.scalar.activation(out=a_sb[t][:], in_=a_ps[t][:], func=ACT.Copy, scale=ga_abs[:, t : t + 1])
            nc.sync.dma_start(out=a_rows[:, t, :], in_=a_sb[t][:])
        for h in range(len(pieces)):
            for t in range(PACK):
                fetch_rival(t, h)
        for c in range(V // P):
            weigh_b(c)
        nc.vector.quantize_mx(out=z2_w[:].bitcast(FP8X4), scales=z2_s[:], in_=z2_bf[:].rearrange("p n t -> p (n t)"))
        for h in range(len(pieces)):
            larger(h)

        scores = [sb.tile([P, V], F32, name=f"scores{r}") for r in range(PACK)]
        first = [sb.tile([P, 2, W], F32, name=f"first{g}") for g in range(2)]
        less_half = [sb.tile([P, 2, W], F32, name=f"less_half{g}") for g in range(2)]
        winner = [sb.tile([P, 2, W], F32, name=f"winner{g}") for g in range(2)]
        result = [sb.tile([P, V], F32, name=f"result{r}") for r in range(PACK)]
        y_bf = sb.tile([P, V, PACK], BF16, name="y_bf", align_bytes=64)
        out_rows = out_0.rearrange("(p r) v -> r p v", r=PACK)

        for r in range(PACK):
            cols = slice(P * r, P * (r + 1))
            nc.vector.quantize_mx(out=z_w[:, cols].bitcast(FP8X4), scales=z_s[:, cols], in_=z_bf[:, r].rearrange("p m t -> p (m t)"))
        for r in range(PACK):
            cols = slice(P * r, P * (r + 1))
            bank = ps.tile([P, V], F32, name=f"s_ps{r}", tag=f"bank{PACK + r}")
            nc.tensor.matmul_mx(out=bank[:], lhsT=z_w[:, cols].bitcast(FP8X4), lhsT_scale=z_s[:, cols],
                                rhs=z2_w[:].bitcast(FP8X4), rhs_scale=z2_s[:], start=True, stop=True)
            nc.scalar.activation(out=scores[r][:], in_=bank[:], func=ACT.Copy, scale=0.0625)
            nc.scalar.activation(out=first[r // 2][:, r % 2, :], in_=scores[r][:].indirect(la_t[:]), func=ACT.Copy)
            if r == 0:
                nc.vector.tensor_scalar(out=less_half[r // 2][:, r % 2, :], in0=scores[r][:].indirect(lb_t[:]), scalar1=-0.5, scalar2=0.0, op0=ALU.mult, op1=ALU.add)
            else:
                nc.scalar.activation(out=less_half[r // 2][:, r % 2, :], in_=scores[r][:].indirect(lb_t[:]), func=ACT.Copy, scale=-0.5)

        def put_first(r):
            nc.vector.tensor_tensor(out=result[r][:].indirect(la_t[:]), in0=first[r // 2][:, r % 2, :], in1=less_half[r // 2][:, r % 2, :], op=ALU.add)

        def put_second(r):
            nc.vector.tensor_copy(out=result[r][:].indirect(lb_t[:]), in_=winner[r // 2][:, r % 2, :])
            nc.sync.dma_start(out=out_rows[r], in_=result[r][:])
            cols = slice(0, V) if r < 2 else slice(HALF, V)
            nc.scalar.copy(out=y_bf[:, cols, r], in_=result[r][:, cols])

        for g in range(2):
            put_first(2 * g)
            nc.vector.scalar_tensor_tensor(out=winner[g][:], in0=less_half[g][:], scalar=-2.0, in1=first[g][:], op0=ALU.mult, op1=ALU.max)
            put_first(2 * g + 1)
            put_second(2 * g)
            put_second(2 * g + 1)

        y_w = sb.tile([P, V], U32, name="y_w", align_bytes=64)
        y_s = sb.tile([P, V], U8, name="y_s", align_bytes=64)
        halves = [slice(HALF * h, HALF * (h + 1)) for h in range(2)]
        for r in (2, 3):
            nc.vector.tensor_copy(out=y_bf[:, :HALF, r], in_=result[r][:, :HALF])
        for cols in halves:
            nc.vector.quantize_mx(out=y_w[:, cols].bitcast(FP8X4), scales=y_s[:, cols], in_=y_bf[:, cols, :].rearrange("p n t -> p (n t)"))
            nc.sync.dma_start(out=words_of(out_1)[:, cols], in_=y_w[:, cols].bitcast(I32))
        for q in range(4):
            engine = nc.scalar if q % 2 else nc.sync
            engine.dma_start(out=out_2[0, 4 * q : 4 * q + 4, :].bitcast(I32), in_=y_s[32 * q : 32 * q + 4, :].bitcast(I32))
